import numpy as np
import ml_dtypes


def mxq(x, axis, fmt="e4m3"):
    dtype, down = {"e4m3": (ml_dtypes.float8_e4m3fn, 7), "e5m2": (ml_dtypes.float8_e5m2, 14)}[fmt]
    v = np.moveaxis(np.asarray(x, np.float32).astype(ml_dtypes.bfloat16).astype(np.float64), axis, -1)
    blocks = v.reshape(v.shape[:-1] + (-1, 32))
    amax = np.abs(blocks).max(-1, keepdims=True)
    byte = np.maximum(np.where(amax > 0, np.frexp(amax)[1] - 1 + 127, 0) - down, 1)
    scale = np.exp2(byte - 127.0)
    codes = (blocks / scale).astype(np.float32).astype(dtype).astype(np.float64)
    return np.moveaxis((codes * scale).reshape(v.shape), -1, axis)


WIDE = False


def mx_kscale(k):
    if not WIDE:
        return np.ones(k)
    levels = np.array([30, -30])
    if k % 512:
        return np.exp2(np.random.permutation(np.resize(levels, k // 32))).repeat(32)
    a = np.empty((k // 512, 16))
    for p in range(k // 512):
        a[p, :8] = np.random.permutation(np.resize(levels, 8))
        for g in range(8):
            far = levels[np.abs(levels - a[p, g]) >= 10]
            a[p, g + 8] = far[np.random.randint(len(far))]
    return np.exp2(a.ravel()).repeat(32)


def f64(x):
    return np.asarray(x).astype(np.float64)


def striped(idx):
    return np.tile(np.asarray(idx).reshape(-1, 16).T, (8, 1)).astype(np.uint16)


def unstriped(offs):
    return offs[:16].T.reshape(-1).astype(np.int64)


E2M1 = np.array([0.0, 0.5, 1.0, 1.5, 2.0, 3.0, 4.0, 6.0, -0.0, -0.5, -1.0, -1.5, -2.0, -3.0, -4.0, -6.0])


def pack_weight(w, fmt):
    k, n = w.shape
    w = f64(np.asarray(w, np.float32).astype(ml_dtypes.bfloat16)).reshape(k // 32, 32, n)
    amax = np.abs(w).max(1)
    if fmt == "e4m3":
        byte = np.frexp(amax)[1] - 1 + 127 - 7
    else:
        mant, ex = np.frexp(amax / 6.0)
        byte = np.where(mant > 0.5, ex, ex - 1) + 127
    byte = np.clip(np.where(amax > 0, byte, 1), 1, 254)
    scaled = (w * np.exp2(127.0 - byte)[:, None, :]).reshape(k, n).astype(np.float32)
    by_word = np.ascontiguousarray(scaled.reshape(k // 512, 128, 4, n).transpose(0, 1, 3, 2))
    if fmt == "e4m3":
        words = by_word.astype(ml_dtypes.float8_e4m3fn).view(np.uint8)
    else:
        c = by_word.astype(ml_dtypes.float4_e2m1fn).view(np.uint8) & 0xF
        words = (c[..., 0::2] | (c[..., 1::2] << 4)).reshape(k // 512, 128, 2 * n)
    return np.ascontiguousarray(words), np.ascontiguousarray(byte.astype(np.uint8).reshape(k // 512, 16, n))


def unpack_weight(words, scales, fmt):
    g, _, n = scales.shape
    words = np.ascontiguousarray(words).reshape(g, 128, n, -1)
    if fmt == "e4m3":
        vals = words.view(ml_dtypes.float8_e4m3fn).astype(np.float64)
    else:
        nib = np.empty((g, 128, n, 4), np.uint8)
        nib[..., 0::2] = words & 0xF
        nib[..., 1::2] = words >> 4
        vals = E2M1[nib]
    vals = vals * np.repeat(np.exp2(scales.astype(np.float64) - 127.0), 8, axis=1)[..., None]
    return vals.transpose(0, 1, 3, 2).reshape(g * 512, n)


def bf(x):
    return np.asarray(x, np.float32).astype(ml_dtypes.bfloat16)


def planes(Y):
    r, m = Y.shape
    b = f64(bf(Y)).reshape(r // 32, 32, m)
    amax = np.abs(b).max(1)
    byte = np.clip(np.where(amax > 0, np.frexp(amax)[1] - 1 + 127 - 7, 1), 1, 254)
    codes = (b * np.exp2(127.0 - byte)[:, None, :]).reshape(r, m).astype(np.float32).astype(ml_dtypes.float8_e4m3fn).view(np.uint8)
    words = codes.reshape(r // 512, 128, 4, m).transpose(0, 1, 3, 2)
    return np.ascontiguousarray(words), np.ascontiguousarray(byte.astype(np.uint8).reshape(r // 512, 16, m))


N, K, T, J, I = 512, 512, 1024, 512, 512


def setup_inputs():
    n = np.random.standard_normal
    idx = np.random.permutation(T)[:J]
    idx2 = np.random.permutation(T)[:I]
    fn = mx_kscale(N)
    wap = pack_weight(n((N, K)) * 1 / np.sqrt(N) * fn[:, None], "e4m3")
    wbp = pack_weight(n((N, K)) * 1 / np.sqrt(N) * fn[:, None], "e2m1")
    return {
        "g": (n((N, T)) * np.exp(0.5 * n((1, T))) / fn[:, None]).astype(np.float32),
        "wa_words": wap[0],
        "wa_scales": wap[1],
        "wb_words": wbp[0],
        "wb_scales": wbp[1],
        "ga": (np.random.uniform(0.4, 1.2, (1, J))).astype(np.float32),
        "gb": (np.random.uniform(0.4, 1.2, (1, I))).astype(np.float32),
        "run": (0.3 * n((K, T))).astype(np.float32),
        "offs": striped(idx),
        "offs2": striped(idx2),
    }


def reference(g, wa_words, wa_scales, wb_words, wb_scales, ga, gb, run, offs, offs2):
    idx = unstriped(offs)
    idx2 = unstriped(offs2)
    wau = unpack_weight(wa_words, wa_scales, "e4m3")
    wbu = unpack_weight(wb_words, wb_scales, "e2m1")
    u = f64(g)[:, idx] * f64(ga)
    v = f64(g)[:, idx2] * f64(gb)
    uq = mxq(u, 0, "e5m2")
    p = wau.T @ uq
    vq = mxq(v, 0, "e5m2")
    q = wbu.T @ vq
    pg = np.zeros((K, T))
    pg[:, idx] = p
    qg = np.zeros((K, T))
    qg[:, idx2] = q
    y = pg + qg + f64(run)
    words, scales = planes(y)
    return y, words, scales

@@ -1,0 +1,258 @@
+from contextlib import ExitStack
+
+import concourse.mybir as mybir
+from concourse.masks import make_identity
+
+N, K, T, J = 512, 512, 1024, 512
+FLOPS = 2 * 2 * N * K * J
+
+F32 = mybir.dt.float32
+BF16 = mybir.dt.bfloat16
+I32 = mybir.dt.int32
+U32 = mybir.dt.uint32
+U16 = mybir.dt.uint16
+U8 = mybir.dt.uint8
+E4M3X4 = mybir.dt.float8_e4m3fn_x4
+E5M2X4 = mybir.dt.float8_e5m2_x4
+E2M1X4 = mybir.dt.float4_e2m1fn_x4
+MULT = mybir.AluOpType.mult
+ADD = mybir.AluOpType.add
+
+P = 128
+PACK = 4
+HALF = T // 2
+BLOCKS = HALF // P
+
+
+def tile_moe_experts_input_gradient_two_pl_kernel(
+    tc, g, wa_words, wa_scales, wb_words, wb_scales, ga, gb, run, offs, offs2, out_0, out_1, out_2
+):
+    nc = tc.nc
+    with ExitStack() as ctx:
+        sb = ctx.enter_context(tc.tile_pool(name="sb", bufs=1))
+        ps = ctx.enter_context(tc.psum_pool(name="ps", bufs=1))
+
+        g_rows = g.rearrange("(p r) c -> p r c", r=PACK)
+        run_rows = run.rearrange("(p r) c -> p r c", r=PACK)
+        out_rows = out_0.rearrange("(p r) c -> p r c", r=PACK)
+        out_words = out_1[0].rearrange("p c r -> p (c r)").bitcast(I32)
+
+        list_a = sb.tile([P, J // 16], U16, name="list_a")
+        list_b = sb.tile([P, J // 16], U16, name="list_b")
+        nc.sync.dma_start(list_a[:], offs)
+        gate_col_a = sb.tile([P, PACK], F32, name="gate_col_a")
+        gate_col_b = sb.tile([P, PACK], F32, name="gate_col_b")
+        nc.scalar.dma_start(gate_col_a[:], ga[0].rearrange("(q b) -> q b", b=PACK))
+        nc.scalar.dma_start(gate_col_b[:], gb[0].rearrange("(q b) -> q b", b=PACK))
+        g_plane = []
+        for r in range(PACK):
+            tile = sb.tile([P, T], F32, name="g_plane%d" % r)
+            nc.sync.dma_start(tile[:], g_rows[:, r, :])
+            g_plane.append(tile)
+        nc.sync.dma_start(list_b[:], offs2)
+
+        wa_raw = sb.tile([P, K], I32, name="wa_raw")
+        nc.sync.dma_start(wa_raw[:], wa_words[0].rearrange("p c r -> p (c r)").bitcast(I32))
+        wb_raw = sb.tile([P, 2 * K], U8, name="wb_raw")
+        nc.sync.dma_start(wb_raw[:].bitcast(I32), wb_words[0].bitcast(I32))
+        ws_raw = sb.tile([P, 2 * K], U8, name="ws_raw")
+        nc.gpsimd.memset(ws_raw[:].bitcast(I32), 0)
+        for e, scales in enumerate((wa_scales, wb_scales)):
+            for q in range(4):
+                nc.sync.dma_start(
+                    ws_raw[32 * q : 32 * q + 4, e * K : (e + 1) * K].bitcast(I32),
+                    scales[0][4 * q : 4 * q + 4, :].bitcast(I32),
+                )
+        run_plane = {}
+        for r in (3, 0, 1, 2):
+            tile = sb.tile([P, T], F32, name="run_plane%d" % r)
+            nc.sync.dma_start(tile[:], run_rows[:, r, :])
+            run_plane[r] = tile
+
+        ident = sb.tile([P, P], F32, name="ident")
+        make_identity(nc, ident[:])
+
+        window = {}
+        for e in range(2):
+            for i in range(2):
+                tile = sb.tile([P, T], F32, name="window%d_%d" % (e, i))
+                nc.vector.memset(tile[:], 0.0)
+                window[(e, i)] = tile
+
+        def spread_gate(col, e, tag):
+            bank = ps.tile([P, PACK, P], F32, name="gate_bank%d" % e, tag="mm%d" % e)
+            for b in range(PACK):
+                nc.tensor.transpose(bank[:, b, :], col[:, b : b + 1].to_broadcast([P, P]), ident[:])
+            gate = sb.tile([P, J], F32, name="gate%d" % e, tag=tag, align_bytes=64)
+            nc.scalar.copy(gate[:].rearrange("p (q b) -> p q b", b=PACK), bank[:].rearrange("p b q -> p q b"))
+            return gate
+
+        gate_a = spread_gate(gate_col_a, 0, "chain0")
+        gate_b = spread_gate(gate_col_b, 1, "gate_b")
+
+        def gather(dst, r, offsets, gate):
+            nc.vector.tensor_tensor(dst, g_plane[r][:].indirect(offsets[:]), gate[:], MULT)
+
+        def quantise(name, src, fmt):
+            codes = sb.tile([P, J], U32, name=name + "_codes", align_bytes=64)
+            scales = sb.tile([P, J], U8, name=name + "_scales", align_bytes=64)
+            nc.vector.quantize_mx(
+                out=codes[:].bitcast(fmt), scales=scales[:], in_=src[:].rearrange("p c r -> p (c r)")
+            )
+            return codes, scales
+
+        u32 = sb.tile([P, PACK, J], F32, name="u32")
+        for r in range(PACK):
+            gather(u32[:, r, :], r, list_a, gate_a)
+        u16 = sb.tile([P, J, PACK], BF16, name="u16", tag="chain1", align_bytes=64)
+        nc.scalar.copy(
+            u16[:].rearrange("p (c i) r -> p c r i", i=4), u32[:].rearrange("p r (c i) -> p c r i", i=4)
+        )
+        v32_lo = sb.tile([P, 2, J], F32, name="v32_lo", tag="chain0", align_bytes=64)
+        for r in range(2):
+            gather(v32_lo[:, r, :], r, list_b, gate_b)
+
+        wa = sb.tile([P, K], I32, name="wa", align_bytes=64)
+        nc.vector.tensor_copy(
+            wa[:].rearrange("p (r m) -> p m r", r=PACK), wa_raw[:].rearrange("p (m r) -> p m r", r=PACK)
+        )
+        wb = sb.tile([P, 2 * K], U8, name="wb", align_bytes=64)
+        nc.vector.tensor_copy(
+            wb[:].bitcast(U16).rearrange("p (r m) -> p m r", r=PACK),
+            wb_raw[:].bitcast(U16).rearrange("p (m r) -> p m r", r=PACK),
+        )
+        ws = sb.tile([P, 2 * K], U8, name="ws", align_bytes=64)
+        nc.vector.tensor_copy(
+            ws[:].rearrange("p (e r m) -> p e m r", e=2, r=PACK),
+            ws_raw[:].rearrange("p (e m r) -> p e m r", e=2, r=PACK),
+        )
+
+        v16 = sb.tile([P, J, PACK], BF16, name="v16", align_bytes=64)
+        nc.scalar.copy(v16[:, :, 0:2], v32_lo[:].rearrange("p r c -> p c r"))
+
+        u_codes, u_scales = quantise("u", u16, E5M2X4)
+
+        v32_hi = sb.tile([P, 2, J], F32, name="v32_hi", tag="chain1", align_bytes=64)
+        for r in range(2):
+            gather(v32_hi[:, r, :], 2 + r, list_b, gate_b)
+
+        operands = {0: (u_codes, u_scales)}
+
+        def product(e, r, bank_tag, src_tag):
+            codes, scales = operands[e]
+            bank = ps.tile([P, J], F32, name="prod%d_%d" % (e, r), tag=bank_tag)
+            if e == 0:
+                lhs = wa[:, r * P : (r + 1) * P].bitcast(E4M3X4)
+            else:
+                lhs = wb[:, 2 * r * P : 2 * (r + 1) * P].bitcast(E2M1X4)
+            nc.tensor.matmul_mx(
+                out=bank[:],
+                lhsT=lhs,
+                lhsT_scale=ws[:, e * K + r * P : e * K + (r + 1) * P],
+                rhs=codes[:].bitcast(E5M2X4),
+                rhs_scale=scales[:],
+                start=True,
+                stop=True,
+            )
+            src = sb.tile([P, J], F32, name="src%d_%d" % (e, r), tag=src_tag, align_bytes=64)
+            nc.scalar.copy(src[:], bank[:])
+            return src
+
+        def scatter(e, i, src):
+            offsets = (list_a, list_b)[e]
+            nc.vector.tensor_copy(window[(e, i)][:].indirect(offsets[:]), src[:])
+
+        def turn_add(banks, term, first, last):
+            for h in range(2):
+                for c in range(BLOCKS):
+                    lo = h * HALF + c * P
+                    nc.tensor.matmul(
+                        banks[h][:, c, :],
+                        term[:, lo : lo + P],
+                        ident[:],
+                        start=(first and c == 0),
+                        stop=(last and c == BLOCKS - 1),
+                        is_transpose=True,
+                    )
+
+        def sum_banks(r):
+            return [ps.tile([P, BLOCKS, P], F32, name="sum%d_%d" % (r, h), tag="sum%d" % h) for h in range(2)]
+
+        def turn_back(r, banks, back_tag):
+            back = []
+            for h in range(2):
+                turned = sb.tile([P, BLOCKS, P], F32, name="turned%d_%d" % (r, h), tag="turned%d" % h)
+                nc.scalar.copy(turned[:], banks[h][:])
+                bank = ps.tile([P, BLOCKS, P], F32, name="back%d_%d" % (r, h), tag="%s%d" % (back_tag, h))
+                for c in range(BLOCKS):
+                    nc.tensor.transpose(bank[:, c, :], turned[:, c, :], ident[:])
+                back.append(bank)
+            return back
+
+        y32 = {}
+        for pair in range(2):
+            for h in range(2):
+                y32[(pair, h)] = sb.tile([P, 2, HALF], F32, name="y32_%d_%d" % (pair, h))
+        y16 = [sb.tile([P, HALF, PACK], BF16, name="y16_%d" % h, align_bytes=64) for h in range(2)]
+
+        def store_y(r, h):
+            nc.sync.dma_start(out_rows[:, r, h * HALF : (h + 1) * HALF], y32[(r // 2, h)][:, r % 2, :])
+
+        src = {}
+        src[(0, 3)] = product(0, 3, "mm0", "src_a3")
+        nc.scalar.copy(v16[:, :, 2:4], v32_hi[:].rearrange("p r c -> p c r"))
+        scatter(0, 0, src[(0, 3)])
+        operands[1] = quantise("v", v16, E5M2X4)
+        src[(0, 0)] = product(0, 0, "mm1", "chain1")
+        banks = sum_banks(3)
+        turn_add(banks, run_plane[3], True, False)
+        src[(1, 0)] = product(1, 0, "mm0", "src_b0")
+        turn_add(banks, window[(0, 0)], False, True)
+        src[(0, 1)] = product(0, 1, "mm1", "src_a1")
+        held = turn_back(3, banks, "held")
+        src[(1, 1)] = product(1, 1, "mm0", "src_b1")
+        src[(0, 2)] = product(0, 2, "mm1", "src_a2")
+        src[(1, 2)] = product(1, 2, "mm0", "src_b2")
+        src_last = product(1, 3, "mm1", "src_b3")
+
+        for r in range(3):
+            banks = sum_banks(r)
+            turn_add(banks, run_plane[r], True, False)
+            scatter(0, (r + 1) % 2, src[(0, r)])
+            turn_add(banks, window[(0, (r + 1) % 2)], False, False)
+            scatter(1, r % 2, src[(1, r)])
+            turn_add(banks, window[(1, r % 2)], False, True)
+            back = turn_back(r, banks, "back")
+            for h in range(2):
+                nc.scalar.copy(y32[(r // 2, h)][:, r % 2, :], back[h][:].rearrange("p c q -> p (c q)"))
+                store_y(r, h)
+            if r == 1:
+                for h in range(2):
+                    nc.scalar.copy(y16[h][:, :, 0:2], y32[(0, h)][:].rearrange("p r c -> p c r"))
+
+        scatter(1, 1, src_last)
+        for h in range(2):
+            nc.vector.tensor_tensor(
+                y32[(1, h)][:, 1, :],
+                held[h][:].rearrange("p c q -> p (c q)"),
+                window[(1, 1)][:, h * HALF : (h + 1) * HALF],
+                ADD,
+            )
+            store_y(3, h)
+        nc.scalar.copy(y16[0][:, :, 2:4], y32[(1, 0)][:].rearrange("p r c -> p c r"))
+        nc.vector.tensor_copy(y16[1][:, :, 2:4], y32[(1, 1)][:].rearrange("p r c -> p c r"))
+
+        y_scales = sb.tile([P, T], U8, name="y_scales", align_bytes=64)
+        for h in (1, 0):
+            y_codes = sb.tile([P, HALF], U32, name="y_codes%d" % h, align_bytes=64)
+            nc.vector.quantize_mx(
+                out=y_codes[:].bitcast(E4M3X4),
+                scales=y_scales[:, h * HALF : (h + 1) * HALF],
+                in_=y16[h][:].rearrange("p c r -> p (c r)"),
+            )
+            nc.sync.dma_start(out_words[:, h * HALF : (h + 1) * HALF], y_codes[:].bitcast(I32))
+        for q in range(4):
+            queue = nc.scalar if q % 2 == 0 else nc.sync
+            queue.dma_start(
+                out_2[0][4 * q : 4 * q + 4, :].bitcast(I32), y_scales[32 * q : 32 * q + 4, :].bitcast(I32)
+            )

@@ -51,9 +51,9 @@ def tile_moe_experts_input_gradient_two_pl_kernel(
             g_plane.append(tile)
         nc.sync.dma_start(list_b[:], offs2)
 
-        wa_raw = sb.tile([P, K], I32, name="wa_raw")
+        wa_raw = sb.tile([P, K], I32, name="wa_raw", tag="chain2", align_bytes=64)
         nc.sync.dma_start(wa_raw[:], wa_words[0].rearrange("p c r -> p (c r)").bitcast(I32))
-        wb_raw = sb.tile([P, 2 * K], U8, name="wb_raw")
+        wb_raw = sb.tile([P, 2 * K], U8, name="wb_raw", tag="chain3", align_bytes=64)
         nc.sync.dma_start(wb_raw[:].bitcast(I32), wb_words[0].bitcast(I32))
         ws_raw = sb.tile([P, 2 * K], U8, name="ws_raw")
         nc.gpsimd.memset(ws_raw[:].bitcast(I32), 0)
@@ -76,7 +76,7 @@ def tile_moe_experts_input_gradient_two_pl_kernel(
         for e in range(2):
             for i in range(2):
                 tile = sb.tile([P, T], F32, name="window%d_%d" % (e, i))
-                nc.vector.memset(tile[:], 0.0)
+                nc.gpsimd.memset(tile[:], 0.0)
                 window[(e, i)] = tile
 
         def spread_gate(col, e, tag):
@@ -101,36 +101,36 @@ def tile_moe_experts_input_gradient_two_pl_kernel(
             )
             return codes, scales
 
-        u32 = sb.tile([P, PACK, J], F32, name="u32")
+        u32 = sb.tile([P, PACK, J], F32, name="u32", tag="chain4", align_bytes=64)
         for r in range(PACK):
             gather(u32[:, r, :], r, list_a, gate_a)
         u16 = sb.tile([P, J, PACK], BF16, name="u16", tag="chain1", align_bytes=64)
         nc.scalar.copy(
             u16[:].rearrange("p (c i) r -> p c r i", i=4), u32[:].rearrange("p r (c i) -> p c r i", i=4)
         )
-        v32_lo = sb.tile([P, 2, J], F32, name="v32_lo", tag="chain0", align_bytes=64)
-        for r in range(2):
-            gather(v32_lo[:, r, :], r, list_b, gate_b)
-
-        wa = sb.tile([P, K], I32, name="wa", align_bytes=64)
+        wa = sb.tile([P, K], I32, name="wa", tag="chain0", align_bytes=64)
         nc.vector.tensor_copy(
             wa[:].rearrange("p (r m) -> p m r", r=PACK), wa_raw[:].rearrange("p (m r) -> p m r", r=PACK)
         )
-        wb = sb.tile([P, 2 * K], U8, name="wb", align_bytes=64)
+        wb = sb.tile([P, 2 * K], U8, name="wb", tag="chain2", align_bytes=64)
         nc.vector.tensor_copy(
             wb[:].bitcast(U16).rearrange("p (r m) -> p m r", r=PACK),
             wb_raw[:].bitcast(U16).rearrange("p (m r) -> p m r", r=PACK),
         )
-        ws = sb.tile([P, 2 * K], U8, name="ws", align_bytes=64)
-        nc.vector.tensor_copy(
-            ws[:].rearrange("p (e r m) -> p e m r", e=2, r=PACK),
-            ws_raw[:].rearrange("p (e m r) -> p e m r", e=2, r=PACK),
-        )
+        v32_lo = sb.tile([P, 2, J], F32, name="v32_lo", tag="chain3", align_bytes=64)
+        for r in range(2):
+            gather(v32_lo[:, r, :], r, list_b, gate_b)
 
         v16 = sb.tile([P, J, PACK], BF16, name="v16", align_bytes=64)
         nc.scalar.copy(v16[:, :, 0:2], v32_lo[:].rearrange("p r c -> p c r"))
 
         u_codes, u_scales = quantise("u", u16, E5M2X4)
+        ws = sb.tile([P, 2 * K], U8, name="ws", tag="chain4", align_bytes=64)
+        nc.vector.tensor_copy(
+            ws[:].rearrange("p (e r m) -> p e m r", e=2, r=PACK),
+            ws_raw[:].rearrange("p (e m r) -> p e m r", e=2, r=PACK),
+        )
+
 
         v32_hi = sb.tile([P, 2, J], F32, name="v32_hi", tag="chain1", align_bytes=64)
         for r in range(2):

@@ -40,55 +40,55 @@ def tile_moe_experts_input_gradient_two_pl_kernel(
         list_a = sb.tile([P, J // 16], U16, name="list_a")
         list_b = sb.tile([P, J // 16], U16, name="list_b")
         nc.sync.dma_start(list_a[:], offs)
-        gate_col_a = sb.tile([P, PACK], F32, name="gate_col_a")
-        gate_col_b = sb.tile([P, PACK], F32, name="gate_col_b")
-        nc.scalar.dma_start(gate_col_a[:], ga[0].rearrange("(q b) -> q b", b=PACK))
-        nc.scalar.dma_start(gate_col_b[:], gb[0].rearrange("(q b) -> q b", b=PACK))
+        gate_col_a = sb.tile([P, 2, 2], F32, name="gate_col_a")
+        gate_col_b = sb.tile([P, 2, 2], F32, name="gate_col_b")
+        nc.scalar.dma_start(gate_col_a[:], ga[0].rearrange("(h q b) -> q h b", h=2, b=2))
+        nc.scalar.dma_start(gate_col_b[:], gb[0].rearrange("(h q b) -> q h b", h=2, b=2))
         g_plane = []
         for r in range(PACK):
-            tile = sb.tile([P, T], F32, name="g_plane%d" % r)
+            tile = sb.tile([P, T], F32, name="g_plane%d" % r, tag="plane%d" % r, align_bytes=64)
             nc.sync.dma_start(tile[:], g_rows[:, r, :])
             g_plane.append(tile)
         nc.sync.dma_start(list_b[:], offs2)
 
         wa_raw = sb.tile([P, K], I32, name="wa_raw", tag="chain2", align_bytes=64)
         nc.sync.dma_start(wa_raw[:], wa_words[0].rearrange("p c r -> p (c r)").bitcast(I32))
-        wb_raw = sb.tile([P, 2 * K], U8, name="wb_raw", tag="chain3", align_bytes=64)
+        wb_raw = sb.tile([P, 2 * K], U8, name="wb_raw")
         nc.sync.dma_start(wb_raw[:].bitcast(I32), wb_words[0].bitcast(I32))
-        ws_raw = sb.tile([P, 2 * K], U8, name="ws_raw")
+        ws_raw = sb.tile([P, K], U8, name="ws_raw")
         nc.gpsimd.memset(ws_raw[:].bitcast(I32), 0)
         for e, scales in enumerate((wa_scales, wb_scales)):
             for q in range(4):
                 nc.sync.dma_start(
-                    ws_raw[32 * q : 32 * q + 4, e * K : (e + 1) * K].bitcast(I32),
+                    ws_raw[32 * q + 4 * e : 32 * q + 4 * e + 4, :].bitcast(I32),
                     scales[0][4 * q : 4 * q + 4, :].bitcast(I32),
                 )
-        run_plane = {}
-        for r in (3, 0, 1, 2):
-            tile = sb.tile([P, T], F32, name="run_plane%d" % r)
-            nc.sync.dma_start(tile[:], run_rows[:, r, :])
-            run_plane[r] = tile
 
         ident = sb.tile([P, P], F32, name="ident")
         make_identity(nc, ident[:])
 
-        window = {}
+        sb_plane = sb.tile([P, K], U8, name="sb_plane", align_bytes=64)
+        nc.gpsimd.memset(sb_plane[:].bitcast(I32), 0)
+        window = []
         for e in range(2):
-            for i in range(2):
-                tile = sb.tile([P, T], F32, name="window%d_%d" % (e, i))
-                nc.gpsimd.memset(tile[:], 0.0)
-                window[(e, i)] = tile
+            tile = sb.tile([P, T], F32, name="window%d" % e)
+            nc.gpsimd.memset(tile[:], 0.0)
+            window.append(tile)
 
-        def spread_gate(col, e, tag):
-            bank = ps.tile([P, PACK, P], F32, name="gate_bank%d" % e, tag="mm%d" % e)
-            for b in range(PACK):
-                nc.tensor.transpose(bank[:, b, :], col[:, b : b + 1].to_broadcast([P, P]), ident[:])
+        def spread_gate(col, e, tag, bank_tag, engines):
             gate = sb.tile([P, J], F32, name="gate%d" % e, tag=tag, align_bytes=64)
-            nc.scalar.copy(gate[:].rearrange("p (q b) -> p q b", b=PACK), bank[:].rearrange("p b q -> p q b"))
+            for h in range(2):
+                bank = ps.tile([P, 2, P], F32, name="gate_bank%d_%d" % (e, h), tag="%s%d" % (bank_tag, h))
+                for b in range(2):
+                    nc.tensor.transpose(bank[:, b, :], col[:, h, b : b + 1].to_broadcast([P, P]), ident[:])
+                engines[h](
+                    gate[:, h * 2 * P : (h + 1) * 2 * P].rearrange("p (q b) -> p q b", b=2),
+                    bank[:].rearrange("p b q -> p q b"),
+                )
             return gate
 
-        gate_a = spread_gate(gate_col_a, 0, "chain0")
-        gate_b = spread_gate(gate_col_b, 1, "gate_b")
+        gate_a = spread_gate(gate_col_a, 0, "chain0", "mm", (nc.scalar.copy, nc.vector.tensor_copy))
+        gate_b = spread_gate(gate_col_b, 1, "gate_b", "sum", (nc.scalar.copy, nc.scalar.copy))
 
         def gather(dst, r, offsets, gate):
             nc.vector.tensor_tensor(dst, g_plane[r][:].indirect(offsets[:]), gate[:], MULT)
@@ -112,35 +112,38 @@ def tile_moe_experts_input_gradient_two_pl_kernel(
         nc.vector.tensor_copy(
             wa[:].rearrange("p (r m) -> p m r", r=PACK), wa_raw[:].rearrange("p (m r) -> p m r", r=PACK)
         )
-        wb = sb.tile([P, 2 * K], U8, name="wb", tag="chain2", align_bytes=64)
-        nc.vector.tensor_copy(
-            wb[:].bitcast(U16).rearrange("p (r m) -> p m r", r=PACK),
-            wb_raw[:].bitcast(U16).rearrange("p (m r) -> p m r", r=PACK),
-        )
-        v32_lo = sb.tile([P, 2, J], F32, name="v32_lo", tag="chain3", align_bytes=64)
+        v32_lo = sb.tile([P, 2, J], F32, name="v32_lo", tag="chain2", align_bytes=64)
         for r in range(2):
             gather(v32_lo[:, r, :], r, list_b, gate_b)
+
+        sa_plane = sb.tile([P, K], U8, name="sa_plane", tag="plane0", align_bytes=64)
+        nc.vector.tensor_copy(
+            sa_plane[:].rearrange("p (r m) -> p m r", r=PACK), ws_raw[:].rearrange("p (m r) -> p m r", r=PACK)
+        )
+        for q in range(4):
+            nc.sync.dma_start(
+                sb_plane[32 * q : 32 * q + 4, :].bitcast(I32), sa_plane[32 * q + 4 : 32 * q + 8, :].bitcast(I32)
+            )
 
         v16 = sb.tile([P, J, PACK], BF16, name="v16", align_bytes=64)
         nc.scalar.copy(v16[:, :, 0:2], v32_lo[:].rearrange("p r c -> p c r"))
 
         u_codes, u_scales = quantise("u", u16, E5M2X4)
-        ws = sb.tile([P, 2 * K], U8, name="ws", tag="chain4", align_bytes=64)
-        nc.vector.tensor_copy(
-            ws[:].rearrange("p (e r m) -> p e m r", e=2, r=PACK),
-            ws_raw[:].rearrange("p (e m r) -> p e m r", e=2, r=PACK),
-        )
-
-
         v32_hi = sb.tile([P, 2, J], F32, name="v32_hi", tag="chain1", align_bytes=64)
         for r in range(2):
             gather(v32_hi[:, r, :], 2 + r, list_b, gate_b)
 
+        run_plane = []
+        for r in range(PACK):
+            tile = sb.tile([P, T], F32, name="run_plane%d" % r, tag="chain4" if r == 0 else "plane%d" % r, align_bytes=64)
+            nc.sync.dma_start(tile[:], run_rows[:, r, :])
+            run_plane.append(tile)
+
         operands = {0: (u_codes, u_scales)}
 
-        def product(e, r, bank_tag, src_tag):
+        def product(e, r):
             codes, scales = operands[e]
-            bank = ps.tile([P, J], F32, name="prod%d_%d" % (e, r), tag=bank_tag)
+            bank = ps.tile([P, J], F32, name="prod%d_%d" % (e, r), tag="mm%d" % ((e + r) % 2))
             if e == 0:
                 lhs = wa[:, r * P : (r + 1) * P].bitcast(E4M3X4)
             else:
@@ -148,19 +151,22 @@ def tile_moe_experts_input_gradient_two_pl_kernel(
             nc.tensor.matmul_mx(
                 out=bank[:],
                 lhsT=lhs,
-                lhsT_scale=ws[:, e * K + r * P : e * K + (r + 1) * P],
+                lhsT_scale=(sa_plane, sb_plane)[e][:, r * P : (r + 1) * P],
                 rhs=codes[:].bitcast(E5M2X4),
                 rhs_scale=scales[:],
                 start=True,
                 stop=True,
             )
-            src = sb.tile([P, J], F32, name="src%d_%d" % (e, r), tag=src_tag, align_bytes=64)
-            nc.scalar.copy(src[:], bank[:])
+            return bank
+
+        def leave_bank(bank, name, tag, lo, hi):
+            src = sb.tile([P, hi - lo], F32, name=name, tag=tag, align_bytes=64)
+            nc.scalar.copy(src[:], bank[:, lo:hi])
             return src
 
-        def scatter(e, i, src):
+        def scatter(e, src, lo, hi):
             offsets = (list_a, list_b)[e]
-            nc.vector.tensor_copy(window[(e, i)][:].indirect(offsets[:]), src[:])
+            nc.vector.tensor_copy(window[e][:].indirect(offsets[:, lo // 16 : hi // 16]), src[:])
 
         def turn_add(banks, term, first, last):
             for h in range(2):
@@ -175,8 +181,11 @@ def tile_moe_experts_input_gradient_two_pl_kernel(
                         is_transpose=True,
                     )
 
-        def sum_banks(r):
-            return [ps.tile([P, BLOCKS, P], F32, name="sum%d_%d" % (r, h), tag="sum%d" % h) for h in range(2)]
+        def open_sum(r):
+            tag = "sum"
+            banks = [ps.tile([P, BLOCKS, P], F32, name="sum%d_%d" % (r, h), tag="%s%d" % (tag, h)) for h in range(2)]
+            turn_add(banks, run_plane[r], True, False)
+            return banks
 
         def turn_back(r, banks, back_tag):
             back = []
@@ -193,64 +202,86 @@ def tile_moe_experts_input_gradient_two_pl_kernel(
         for pair in range(2):
             for h in range(2):
                 y32[(pair, h)] = sb.tile([P, 2, HALF], F32, name="y32_%d_%d" % (pair, h))
-        y16 = [sb.tile([P, HALF, PACK], BF16, name="y16_%d" % h, align_bytes=64) for h in range(2)]
+        parts = ((0, HALF // 2), (HALF // 2, HALF // 2), (HALF, HALF))
+        y16 = [sb.tile([P, w, PACK], BF16, name="y16_%d" % lo, align_bytes=64) for lo, w in parts]
+
+        def round_pair(copy, pair, i):
+            lo, w = parts[i]
+            h = lo // HALF
+            copy(
+                y16[i][:, :, 2 * pair : 2 * pair + 2],
+                y32[(pair, h)][:, :, lo - h * HALF : lo - h * HALF + w].rearrange("p r c -> p c r"),
+            )
 
         def store_y(r, h):
             nc.sync.dma_start(out_rows[:, r, h * HALF : (h + 1) * HALF], y32[(r // 2, h)][:, r % 2, :])
 
-        src = {}
-        src[(0, 3)] = product(0, 3, "mm0", "src_a3")
-        nc.scalar.copy(v16[:, :, 2:4], v32_hi[:].rearrange("p r c -> p c r"))
-        scatter(0, 0, src[(0, 3)])
-        operands[1] = quantise("v", v16, E5M2X4)
-        src[(0, 0)] = product(0, 0, "mm1", "chain1")
-        banks = sum_banks(3)
-        turn_add(banks, run_plane[3], True, False)
-        src[(1, 0)] = product(1, 0, "mm0", "src_b0")
-        turn_add(banks, window[(0, 0)], False, True)
-        src[(0, 1)] = product(0, 1, "mm1", "src_a1")
-        held = turn_back(3, banks, "held")
-        src[(1, 1)] = product(1, 1, "mm0", "src_b1")
-        src[(0, 2)] = product(0, 2, "mm1", "src_a2")
-        src[(1, 2)] = product(1, 2, "mm0", "src_b2")
-        src_last = product(1, 3, "mm1", "src_b3")
-
-        for r in range(3):
-            banks = sum_banks(r)
-            turn_add(banks, run_plane[r], True, False)
-            scatter(0, (r + 1) % 2, src[(0, r)])
-            turn_add(banks, window[(0, (r + 1) % 2)], False, False)
-            scatter(1, r % 2, src[(1, r)])
-            turn_add(banks, window[(1, r % 2)], False, True)
+        def finish(r, banks):
             back = turn_back(r, banks, "back")
             for h in range(2):
                 nc.scalar.copy(y32[(r // 2, h)][:, r % 2, :], back[h][:].rearrange("p c q -> p (c q)"))
                 store_y(r, h)
-            if r == 1:
-                for h in range(2):
-                    nc.scalar.copy(y16[h][:, :, 0:2], y32[(0, h)][:].rearrange("p r c -> p c r"))
 
-        scatter(1, 1, src_last)
+        bank = product(0, 0)
+        first = leave_bank(bank, "src_first", "src_first", 0, J // 2)
+        nc.scalar.copy(v16[:, :, 2:4], v32_hi[:].rearrange("p r c -> p c r"))
+        scatter(0, first, 0, J // 2)
+        wb = sb.tile([P, 2 * K], U8, name="wb", tag="src_first", align_bytes=64)
+        nc.vector.tensor_copy(
+            wb[:].bitcast(U16).rearrange("p (r m) -> p m r", r=PACK),
+            wb_raw[:].bitcast(U16).rearrange("p (m r) -> p m r", r=PACK),
+        )
+        operands[1] = quantise("v", v16, E5M2X4)
+        second = leave_bank(bank, "src_second", "chain1", J // 2, J)
+        scatter(0, second, J // 2, J)
+        src = {}
+
+        def make_source(e, r):
+            name = "src%d_%d" % (e, r)
+            src[(e, r)] = leave_bank(product(e, r), name, name, 0, J)
+
+        make_source(1, 0)
+        make_source(0, 1)
+        make_source(1, 1)
+        for r in range(PACK):
+            banks = open_sum(r)
+            if r > 0:
+                scatter(0, src[(0, r)], 0, J)
+            turn_add(banks, window[0], False, r == PACK - 1)
+            scatter(1, src[(1, r)], 0, J)
+            if r < PACK - 1:
+                turn_add(banks, window[1], False, True)
+                finish(r, banks)
+            if r + 2 < PACK:
+                make_source(0, r + 2)
+                make_source(1, r + 2)
+            if r == 1:
+                for i in range(len(parts)):
+                    round_pair(nc.scalar.copy, 0, i)
+        held = turn_back(PACK - 1, banks, "held")
+
         for h in range(2):
             nc.vector.tensor_tensor(
                 y32[(1, h)][:, 1, :],
                 held[h][:].rearrange("p c q -> p (c q)"),
-                window[(1, 1)][:, h * HALF : (h + 1) * HALF],
+                window[1][:, h * HALF : (h + 1) * HALF],
                 ADD,
             )
             store_y(3, h)
-        nc.scalar.copy(y16[0][:, :, 2:4], y32[(1, 0)][:].rearrange("p r c -> p c r"))
-        nc.vector.tensor_copy(y16[1][:, :, 2:4], y32[(1, 1)][:].rearrange("p r c -> p c r"))
+        round_pair(nc.scalar.copy, 1, 0)
+        round_pair(nc.scalar.copy, 1, 1)
+        round_pair(nc.vector.tensor_copy, 1, 2)
 
         y_scales = sb.tile([P, T], U8, name="y_scales", align_bytes=64)
-        for h in (1, 0):
-            y_codes = sb.tile([P, HALF], U32, name="y_codes%d" % h, align_bytes=64)
+        for i in (0, 2, 1):
+            lo, w = parts[i]
+            y_codes = sb.tile([P, w], U32, name="y_codes%d" % i, align_bytes=64)
             nc.vector.quantize_mx(
                 out=y_codes[:].bitcast(E4M3X4),
-                scales=y_scales[:, h * HALF : (h + 1) * HALF],
-                in_=y16[h][:].rearrange("p c r -> p (c r)"),
+                scales=y_scales[:, lo : lo + w],
+                in_=y16[i][:].rearrange("p c r -> p (c r)"),
             )
-            nc.sync.dma_start(out_words[:, h * HALF : (h + 1) * HALF], y_codes[:].bitcast(I32))
+            nc.sync.dma_start(out_words[:, lo : lo + w], y_codes[:].bitcast(I32))
         for q in range(4):
             queue = nc.scalar if q % 2 == 0 else nc.sync
             queue.dma_start(

from contextlib import ExitStack

import concourse.mybir as mybir
from concourse.masks import make_identity

N, K, T, J = 512, 512, 1024, 512
FLOPS = 2 * 2 * N * K * J

F32 = mybir.dt.float32
BF16 = mybir.dt.bfloat16
I32 = mybir.dt.int32
U32 = mybir.dt.uint32
U16 = mybir.dt.uint16
U8 = mybir.dt.uint8
E4M3X4 = mybir.dt.float8_e4m3fn_x4
E5M2X4 = mybir.dt.float8_e5m2_x4
E2M1X4 = mybir.dt.float4_e2m1fn_x4
MULT = mybir.AluOpType.mult
ADD = mybir.AluOpType.add

P = 128
PACK = 4
HALF = T // 2
BLOCKS = HALF // P


def tile_moe_experts_input_gradient_two_pl_kernel(
    tc, g, wa_words, wa_scales, wb_words, wb_scales, ga, gb, run, offs, offs2, out_0, out_1, out_2
):
    nc = tc.nc
    with ExitStack() as ctx:
        sb = ctx.enter_context(tc.tile_pool(name="sb", bufs=1))
        ps = ctx.enter_context(tc.psum_pool(name="ps", bufs=1))

        g_rows = g.rearrange("(p r) c -> p r c", r=PACK)
        run_rows = run.rearrange("(p r) c -> p r c", r=PACK)
        out_rows = out_0.rearrange("(p r) c -> p r c", r=PACK)
        out_words = out_1[0].rearrange("p c r -> p (c r)").bitcast(I32)

        list_a = sb.tile([P, J // 16], U16, name="list_a")
        list_b = sb.tile([P, J // 16], U16, name="list_b")
        nc.sync.dma_start(list_a[:], offs)
        gate_col_a = sb.tile([P, 2, 2], F32, name="gate_col_a")
        gate_col_b = sb.tile([P, 2, 2], F32, name="gate_col_b")
        nc.scalar.dma_start(gate_col_a[:], ga[0].rearrange("(h q b) -> q h b", h=2, b=2))
        nc.scalar.dma_start(gate_col_b[:], gb[0].rearrange("(h q b) -> q h b", h=2, b=2))
        g_plane = []
        for r in range(PACK):
            tile = sb.tile([P, T], F32, name="g_plane%d" % r, tag="plane%d" % r, align_bytes=64)
            nc.sync.dma_start(tile[:], g_rows[:, r, :])
            g_plane.append(tile)
        nc.sync.dma_start(list_b[:], offs2)

        wa_raw = sb.tile([P, K], I32, name="wa_raw", tag="chain2", align_bytes=64)
        nc.sync.dma_start(wa_raw[:], wa_words[0].rearrange("p c r -> p (c r)").bitcast(I32))
        wb_raw = sb.tile([P, 2 * K], U8, name="wb_raw")
        nc.sync.dma_start(wb_raw[:].bitcast(I32), wb_words[0].bitcast(I32))
        ws_raw = sb.tile([P, K], U8, name="ws_raw")
        nc.gpsimd.memset(ws_raw[:].bitcast(I32), 0)
        for e, scales in enumerate((wa_scales, wb_scales)):
            for q in range(4):
                nc.sync.dma_start(
                    ws_raw[32 * q + 4 * e : 32 * q + 4 * e + 4, :].bitcast(I32),
                    scales[0][4 * q : 4 * q + 4, :].bitcast(I32),
                )

        ident = sb.tile([P, P], F32, name="ident")
        make_identity(nc, ident[:])

        sb_plane = sb.tile([P, K], U8, name="sb_plane", align_bytes=64)
        nc.gpsimd.memset(sb_plane[:].bitcast(I32), 0)
        window = []
        for e in range(2):
            tile = sb.tile([P, T], F32, name="window%d" % e)
            nc.gpsimd.memset(tile[:], 0.0)
            window.append(tile)

        def spread_gate(col, e, tag, bank_tag, engines):
            gate = sb.tile([P, J], F32, name="gate%d" % e, tag=tag, align_bytes=64)
            for h in range(2):
                bank = ps.tile([P, 2, P], F32, name="gate_bank%d_%d" % (e, h), tag="%s%d" % (bank_tag, h))
                for b in range(2):
                    nc.tensor.transpose(bank[:, b, :], col[:, h, b : b + 1].to_broadcast([P, P]), ident[:])
                engines[h](
                    gate[:, h * 2 * P : (h + 1) * 2 * P].rearrange("p (q b) -> p q b", b=2),
                    bank[:].rearrange("p b q -> p q b"),
                )
            return gate

        gate_a = spread_gate(gate_col_a, 0, "chain0", "mm", (nc.scalar.copy, nc.vector.tensor_copy))
        gate_b = spread_gate(gate_col_b, 1, "gate_b", "sum", (nc.scalar.copy, nc.scalar.copy))

        def gather(dst, r, offsets, gate):
            nc.vector.tensor_tensor(dst, g_plane[r][:].indirect(offsets[:]), gate[:], MULT)

        def quantise(name, src, fmt):
            codes = sb.tile([P, J], U32, name=name + "_codes", align_bytes=64)
            scales = sb.tile([P, J], U8, name=name + "_scales", align_bytes=64)
            nc.vector.quantize_mx(
                out=codes[:].bitcast(fmt), scales=scales[:], in_=src[:].rearrange("p c r -> p (c r)")
            )
            return codes, scales

        u32 = sb.tile([P, PACK, J], F32, name="u32", tag="chain4", align_bytes=64)
        for r in range(PACK):
            gather(u32[:, r, :], r, list_a, gate_a)
        u16 = sb.tile([P, J, PACK], BF16, name="u16", tag="chain1", align_bytes=64)
        nc.scalar.copy(
            u16[:].rearrange("p (c i) r -> p c r i", i=4), u32[:].rearrange("p r (c i) -> p c r i", i=4)
        )
        wa = sb.tile([P, K], I32, name="wa", tag="chain0", align_bytes=64)
        nc.vector.tensor_copy(
            wa[:].rearrange("p (r m) -> p m r", r=PACK), wa_raw[:].rearrange("p (m r) -> p m r", r=PACK)
        )
        v32_lo = sb.tile([P, 2, J], F32, name="v32_lo", tag="chain2", align_bytes=64)
        for r in range(2):
            gather(v32_lo[:, r, :], r, list_b, gate_b)

        sa_plane = sb.tile([P, K], U8, name="sa_plane", tag="plane0", align_bytes=64)
        nc.vector.tensor_copy(
            sa_plane[:].rearrange("p (r m) -> p m r", r=PACK), ws_raw[:].rearrange("p (m r) -> p m r", r=PACK)
        )
        for q in range(4):
            nc.sync.dma_start(
                sb_plane[32 * q : 32 * q + 4, :].bitcast(I32), sa_plane[32 * q + 4 : 32 * q + 8, :].bitcast(I32)
            )

        v16 = sb.tile([P, J, PACK], BF16, name="v16", align_bytes=64)
        nc.scalar.copy(v16[:, :, 0:2], v32_lo[:].rearrange("p r c -> p c r"))

        u_codes, u_scales = quantise("u", u16, E5M2X4)
        v32_hi = sb.tile([P, 2, J], F32, name="v32_hi", tag="chain1", align_bytes=64)
        for r in range(2):
            gather(v32_hi[:, r, :], 2 + r, list_b, gate_b)

        run_plane = []
        for r in range(PACK):
            tile = sb.tile([P, T], F32, name="run_plane%d" % r, tag="chain4" if r == 0 else "plane%d" % r, align_bytes=64)
            nc.sync.dma_start(tile[:], run_rows[:, r, :])
            run_plane.append(tile)

        operands = {0: (u_codes, u_scales)}

        def product(e, r):
            codes, scales = operands[e]
            bank = ps.tile([P, J], F32, name="prod%d_%d" % (e, r), tag="mm%d" % ((e + r) % 2))
            if e == 0:
                lhs = wa[:, r * P : (r + 1) * P].bitcast(E4M3X4)
            else:
                lhs = wb[:, 2 * r * P : 2 * (r + 1) * P].bitcast(E2M1X4)
            nc.tensor.matmul_mx(
                out=bank[:],
                lhsT=lhs,
                lhsT_scale=(sa_plane, sb_plane)[e][:, r * P : (r + 1) * P],
                rhs=codes[:].bitcast(E5M2X4),
                rhs_scale=scales[:],
                start=True,
                stop=True,
            )
            return bank

        def leave_bank(bank, name, tag, lo, hi):
            src = sb.tile([P, hi - lo], F32, name=name, tag=tag, align_bytes=64)
            nc.scalar.copy(src[:], bank[:, lo:hi])
            return src

        def scatter(e, src, lo, hi):
            offsets = (list_a, list_b)[e]
            nc.vector.tensor_copy(window[e][:].indirect(offsets[:, lo // 16 : hi // 16]), src[:])

        def turn_add(banks, term, first, last):
            for h in range(2):
                for c in range(BLOCKS):
                    lo = h * HALF + c * P
                    nc.tensor.matmul(
                        banks[h][:, c, :],
                        term[:, lo : lo + P],
                        ident[:],
                        start=(first and c == 0),
                        stop=(last and c == BLOCKS - 1),
                        is_transpose=True,
                    )

        def open_sum(r):
            tag = "sum"
            banks = [ps.tile([P, BLOCKS, P], F32, name="sum%d_%d" % (r, h), tag="%s%d" % (tag, h)) for h in range(2)]
            turn_add(banks, run_plane[r], True, False)
            return banks

        def turn_back(r, banks, back_tag):
            back = []
            for h in range(2):
                turned = sb.tile([P, BLOCKS, P], F32, name="turned%d_%d" % (r, h), tag="turned%d" % h)
                nc.scalar.copy(turned[:], banks[h][:])
                bank = ps.tile([P, BLOCKS, P], F32, name="back%d_%d" % (r, h), tag="%s%d" % (back_tag, h))
                for c in range(BLOCKS):
                    nc.tensor.transpose(bank[:, c, :], turned[:, c, :], ident[:])
                back.append(bank)
            return back

        y32 = {}
        for pair in range(2):
            for h in range(2):
                y32[(pair, h)] = sb.tile([P, 2, HALF], F32, name="y32_%d_%d" % (pair, h))
        parts = ((0, HALF // 2), (HALF // 2, HALF // 2), (HALF, HALF))
        y16 = [sb.tile([P, w, PACK], BF16, name="y16_%d" % lo, align_bytes=64) for lo, w in parts]

        def round_pair(copy, pair, i):
            lo, w = parts[i]
            h = lo // HALF
            copy(
                y16[i][:, :, 2 * pair : 2 * pair + 2],
                y32[(pair, h)][:, :, lo - h * HALF : lo - h * HALF + w].rearrange("p r c -> p c r"),
            )

        def store_y(r, h):
            nc.sync.dma_start(out_rows[:, r, h * HALF : (h + 1) * HALF], y32[(r // 2, h)][:, r % 2, :])

        def finish(r, banks):
            back = turn_back(r, banks, "back")
            for h in range(2):
                nc.scalar.copy(y32[(r // 2, h)][:, r % 2, :], back[h][:].rearrange("p c q -> p (c q)"))
                store_y(r, h)

        bank = product(0, 0)
        first = leave_bank(bank, "src_first", "src_first", 0, J // 2)
        nc.scalar.copy(v16[:, :, 2:4], v32_hi[:].rearrange("p r c -> p c r"))
        scatter(0, first, 0, J // 2)
        wb = sb.tile([P, 2 * K], U8, name="wb", tag="src_first", align_bytes=64)
        nc.vector.tensor_copy(
            wb[:].bitcast(U16).rearrange("p (r m) -> p m r", r=PACK),
            wb_raw[:].bitcast(U16).rearrange("p (m r) -> p m r", r=PACK),
        )
        operands[1] = quantise("v", v16, E5M2X4)
        second = leave_bank(bank, "src_second", "chain1", J // 2, J)
        scatter(0, second, J // 2, J)
        src = {}

        def make_source(e, r):
            name = "src%d_%d" % (e, r)
            src[(e, r)] = leave_bank(product(e, r), name, name, 0, J)

        make_source(1, 0)
        make_source(0, 1)
        make_source(1, 1)
        for r in range(PACK):
            banks = open_sum(r)
            if r > 0:
                scatter(0, src[(0, r)], 0, J)
            turn_add(banks, window[0], False, r == PACK - 1)
            scatter(1, src[(1, r)], 0, J)
            if r < PACK - 1:
                turn_add(banks, window[1], False, True)
                finish(r, banks)
            if r + 2 < PACK:
                make_source(0, r + 2)
                make_source(1, r + 2)
            if r == 1:
                for i in range(len(parts)):
                    round_pair(nc.scalar.copy, 0, i)
        held = turn_back(PACK - 1, banks, "held")

        for h in range(2):
            nc.vector.tensor_tensor(
                y32[(1, h)][:, 1, :],
                held[h][:].rearrange("p c q -> p (c q)"),
                window[1][:, h * HALF : (h + 1) * HALF],
                ADD,
            )
            store_y(3, h)
        round_pair(nc.scalar.copy, 1, 0)
        round_pair(nc.scalar.copy, 1, 1)
        round_pair(nc.vector.tensor_copy, 1, 2)

        y_scales = sb.tile([P, T], U8, name="y_scales", align_bytes=64)
        for i in (0, 2, 1):
            lo, w = parts[i]
            y_codes = sb.tile([P, w], U32, name="y_codes%d" % i, align_bytes=64)
            nc.vector.quantize_mx(
                out=y_codes[:].bitcast(E4M3X4),
                scales=y_scales[:, lo : lo + w],
                in_=y16[i][:].rearrange("p c r -> p (c r)"),
            )
            nc.sync.dma_start(out_words[:, lo : lo + w], y_codes[:].bitcast(I32))
        for q in range(4):
            queue = nc.scalar if q % 2 == 0 else nc.sync
            queue.dma_start(
                out_2[0][4 * q : 4 * q + 4, :].bitcast(I32), y_scales[32 * q : 32 * q + 4, :].bitcast(I32)
            )
